import numpy as np, ml_dtypes
CORES = [33,34,161,162,289,290,417,418]
N = 8
import mx_ref
NC = 128
BF = ml_dtypes.bfloat16
def setup_inputs(rng):
    def f(*shape):
        return mx_ref.flush((rng.standard_normal(shape, dtype=np.float32) * np.exp2(rng.integers(-2, 3, shape[:-1] + (1,)))).astype(BF))
    return {"x": f(N, 128, 512), "rt": f(N, 128, 512), "w": f(N, 128, 4 * NC)}
def setup_inputs_blocks(rng):
    d = setup_inputs(rng)
    for k in ("x", "rt", "w"): d[k] = mx_ref.spread(d[k], rng, 1)
    return d
def setup_inputs_wide(rng):
    d = setup_inputs(rng)
    for k in ("x", "rt", "w"): d[k] = mx_ref.flush((d[k].astype(np.float32) * np.exp2(rng.integers(-6, 7, (N, 1, 1))).astype(np.float32)).astype(BF))
    return d
def setup_inputs_near(rng):
    d = setup_inputs(rng); v = d["rt"].astype(np.float32).reshape(N, 128, -1, 4)
    d["rt"] = mx_ref.flush((v[:, :, :1] + v / 64).reshape(d["rt"].shape).astype(BF))
    return d
def setup_inputs_twins(rng):
    d = setup_inputs(rng); v = d["rt"].reshape(N, 128, -1, 4).copy()
    v[:, :, 1] = v[:, :, 0]
    d["rt"] = v.reshape(d["rt"].shape)
    return d
def reference(x, rt, w):
    W = [mx_ref.quantize(w[e]) for e in range(N)]
    y = np.zeros((N, 128, NC), np.float32)
    for j in range(N):
        X = mx_ref.quantize(x[j])
        lg = mx_ref.matmul(X, mx_ref.quantize(rt[j]))[:, :N]
        m = lg.max(axis=1, keepdims=True); m2 = np.where(lg < m, lg, -np.inf).max(axis=1, keepdims=True)
        for e in range(N):
            y[j] = y[j] + (lg[:, e:e + 1] >= m2) * (mx_ref.matmul(X, W[e]) * lg[:, e:e + 1])
    return {"y": y}

@@ -1,0 +1,181 @@
+from concourse.bass import DstId, RemoteDMATransfer
+from concourse.mybir import dt, AluOpType, AxisListType, ActivationFunctionType
+
+NE = 8
+C = 128
+SCRATCH = {
+    "wt": ("sbuf", [128, 512], "bfloat16"),
+    "xt": ("sbuf", [128, 512], "bfloat16"),
+    "rtt": ("sbuf", [128, 512], "bfloat16"),
+    "wq": ("sbuf", [128, NE * C], "float8_e4m3fn_x4"),
+    "ws": ("sbuf", [128, NE * C], "uint8"),
+    "xq": ("sbuf", [128, C], "float8_e4m3fn_x4"),
+    "xs": ("sbuf", [128, C], "uint8"),
+    "rq": ("sbuf", [128, C], "float8_e4m3fn_x4"),
+    "rs": ("sbuf", [128, C], "uint8"),
+    "ps": ("psum", [128, 512 * 8], "float32"),
+    "lg": ("sbuf", [128, NE], "float32"),
+    "pen": ("sbuf", [128, NE], "float32"),
+    "low": ("sbuf", [128, NE], "float32"),
+    "sel": ("sbuf", [128, NE], "float32"),
+    "coef": ("sbuf", [128, NE], "float32"),
+    "m1": ("sbuf", [128, 1], "float32"),
+    "m2": ("sbuf", [128, 1], "float32"),
+    "tmp": ("sbuf", [128, NE * C], "float32"),
+    "acc": ("sbuf", [128, C], "float32"),
+    "yt": ("sbuf", [128, C], "float32"),
+}
+SEMAPHORES = (["lw", "lx", "lr", "qw", "qx", "mr", "lgc", "v", "coef_ok", "yv", "stored", "sent"]
+              + ["c%d" % e for e in range(NE)] + ["p%d" % e for e in range(NE)]
+              + ["m%d" % e for e in range(NE)] + ["a%d" % e for e in range(NE)])
+
+
+def _bits(m):
+    return [i for i in range(m.bit_length()) if (m >> i) & 1]
+
+
+def _mask(bits):
+    return sum(1 << i for i in bits)
+
+
+def _group(T, topo, core):
+    def here(c):
+        return [d for d in T.cores if topo.host(d) == topo.host(c) and topo.chip(d) == topo.chip(c)]
+
+    pos = here(core).index(core)
+    mate = [d for d in here(core) if d != core][0]
+    rack, cable, diag = {}, {}, {}
+    for d in T.cores:
+        if topo.host(d) == topo.host(core):
+            continue
+        p = here(d).index(d)
+        side = "same" if p == pos else "other"
+        if topo.same_plane(core, d):
+            rack[side] = d
+        elif topo.may_write(core, d):
+            cable[side] = d
+        else:
+            diag[side] = d
+    return mate, rack, cable, diag
+
+
+def rank_program(g, core, T, topo):
+    rank = T.rank_of(core)
+    if rank is None:
+        return
+    S = T.sem
+    mate, rack, cable, diag = _group(T, topo, core)
+
+    off = _bits(topo.mask(core, rack["same"]) & topo.mask(core, cable["same"]))
+    on = [i for i in _bits(topo.mask(core, mate)) if i not in off]
+    via_switch, via_cable = off[0::2], off[1::2]
+    mate_a, mate_b = on[0::2], on[1::2]
+
+    own, r, c = rank, T.rank_of(rack["same"]), T.rank_of(cable["same"])
+    ro, co = T.rank_of(rack["other"]), T.rank_of(cable["other"])
+    ds, do, mt = T.rank_of(diag["same"]), T.rank_of(diag["other"]), T.rank_of(mate)
+    codes_due = {mt: len(on), r: len(via_switch), c: len(via_cable), ro: len(on), co: len(on),
+                 ds: len(via_cable), do: len(via_switch)}
+    planes_due = {mt: len(on), r: len(via_switch), c: len(via_cable), ro: len(mate_a), co: len(mate_b),
+                  ds: len(via_cable), do: len(via_switch)}
+
+    def codes(e):
+        return T.wq[:, e * C:(e + 1) * C]
+
+    def plane(e):
+        return T.ws[:, e * C:(e + 1) * C]
+
+    sent = [0]
+
+    def send(kind, moves):
+        ts = []
+        for e, d, engines in moves:
+            rid, pid = topo.addr(d, core)
+            ap = codes(e).bitcast(dt.uint8) if kind == "c" else plane(e)
+            ts.append(RemoteDMATransfer(dst_ids=[DstId(rid=rid, pnc=pid)], dma_engine_mask=_mask(engines),
+                                        remote_sem=S["%s%d" % (kind, e)], src=ap, dst=ap))
+            sent[0] += len(engines)
+        g.remote_dma_fused(ts, local_sem=S.sent)
+
+    g.sync.dma_start(T.wt[:], T.w[:]).then_inc(S.lw, 16)
+    g.sync.dma_start(T.xt[:], T.x[:]).then_inc(S.lx, 16)
+    g.sync.dma_start(T.rtt[:], T.rt[:]).then_inc(S.lr, 16)
+    g.sync.wait_ge(S.yv, 1)
+    g.sync.dma_start(T.y[:], T.yt[:]).then_inc(S.stored, 16)
+    g.sync.wait_ge(S.stored, 16)
+
+    g.wait_ge(S.qw, 1)
+    first = [(own, rack["same"], via_switch), (own, cable["same"], via_cable)]
+    send("c", first)
+    send("p", first)
+    send("c", [(own, mate, on)])
+    send("p", [(own, mate, on)])
+    g.wait_ge(S["c%d" % r], codes_due[r])
+    send("c", [(r, cable["same"], via_cable), (r, mate, on)])
+    g.wait_ge(S["c%d" % c], codes_due[c])
+    send("c", [(c, rack["other"], via_switch), (c, mate, on)])
+    g.wait_ge(S["p%d" % r], planes_due[r])
+    g.wait_ge(S["p%d" % c], planes_due[c])
+    send("p", [(r, cable["same"], via_cable), (c, rack["other"], via_switch), (r, mate, mate_a), (c, mate, mate_b)])
+    g.wait_ge(S.sent, sent[0])
+
+    order = [own, mt, r, c, ro, co, ds, do]
+
+    def bank(k):
+        return 512 * ((k + 1) % 8)
+
+    g.tensor.wait_ge(S.qx, 2)
+    g.tensor.matmul_mx(T.ps[:, 0:C], T.xq[:], T.xs[:], T.rq[:], T.rs[:], True, True).then_inc(S.mr, 1)
+    for k, e in enumerate(order):
+        if e == own:
+            g.tensor.wait_ge(S.qw, 1)
+        else:
+            g.tensor.wait_ge(S["c%d" % e], codes_due[e])
+            g.tensor.wait_ge(S["p%d" % e], planes_due[e])
+        if bank(k) == 0:
+            g.tensor.wait_ge(S.lgc, 1)
+        g.tensor.matmul_mx(T.ps[:, bank(k):bank(k) + C], T.xq[:], T.xs[:], codes(e), plane(e), True, True
+                           ).then_inc(S["m%d" % k], 1)
+
+    V = g.vector
+    V.wait_ge(S.lw, 16)
+    V.quantize_mx(codes(own), plane(own), T.wt[:]).then_inc(S.qw, 1)
+    V.wait_ge(S.lx, 16)
+    V.quantize_mx(T.xq[:], T.xs[:], T.xt[:]).then_inc(S.qx, 1)
+    V.wait_ge(S.lr, 16)
+    V.quantize_mx(T.rq[:], T.rs[:], T.rtt[:]).then_inc(S.qx, 1)
+
+    nv = [0]
+
+    def step(ins):
+        nv[0] += 1
+        ins.then_inc(S.v, 1)
+        V.wait_ge(S.v, nv[0])
+
+    X = AxisListType.X
+    V.wait_ge(S.mr, 1)
+    V.tensor_copy(T.lg[:], T.ps[:, 0:NE]).then_inc(S.lgc, 1)
+    V.wait_ge(S.lgc, 1)
+    step(V.tensor_reduce(T.m1[:], T.lg[:], X, AluOpType.max))
+    step(V.tensor_scalar(T.pen[:], T.lg[:], T.m1[:], -1e29, AluOpType.is_ge, AluOpType.mult))
+    step(V.tensor_tensor(T.low[:], T.lg[:], T.pen[:], AluOpType.add))
+    step(V.tensor_reduce(T.m2[:], T.low[:], X, AluOpType.max))
+    step(V.tensor_scalar(T.sel[:], T.lg[:], T.m2[:], None, AluOpType.is_ge))
+    V.tensor_tensor(T.coef[:], T.sel[:], T.lg[:], AluOpType.mult).then_inc(S.coef_ok, 1)
+
+    def tmp(k):
+        return T.tmp[:, k * C:(k + 1) * C]
+
+    g.scalar.wait_ge(S.coef_ok, 1)
+    for k, e in enumerate(order):
+        g.scalar.wait_ge(S["m%d" % k], 1)
+        g.scalar.activation(tmp(k), T.ps[:, bank(k):bank(k) + C], ActivationFunctionType.Identity,
+                            scale=T.coef[:, e:e + 1]).then_inc(S["a%d" % k], 1)
+    V.wait_ge(S.a0, 1)
+    for k in range(1, NE):
+        V.wait_ge(S["a%d" % k], 1)
+        a = tmp(0) if k == 1 else T.acc[:]
+        if k < NE - 1:
+            step(V.tensor_tensor(T.acc[:], a, tmp(k), AluOpType.add))
+        else:
+            V.tensor_tensor(T.yt[:], a, tmp(k), AluOpType.add).then_inc(S.yv, 1)

@@ -3,6 +3,8 @@ from concourse.mybir import dt, AluOpType, AxisListType, ActivationFunctionType
 
 NE = 8
 C = 128
+LO = 64
+WORLD = 512
 SCRATCH = {
     "wt": ("sbuf", [128, 512], "bfloat16"),
     "xt": ("sbuf", [128, 512], "bfloat16"),
@@ -26,8 +28,7 @@ SCRATCH = {
     "yt": ("sbuf", [128, C], "float32"),
 }
 SEMAPHORES = (["lw", "lx", "lr", "qw", "qx", "mr", "lgc", "v", "coef_ok", "yv", "stored", "sent"]
-              + ["c%d" % e for e in range(NE)] + ["p%d" % e for e in range(NE)]
-              + ["m%d" % e for e in range(NE)] + ["a%d" % e for e in range(NE)])
+              + ["%s%d" % (k, e) for k in "chpma" for e in range(NE)])
 
 
 def _bits(m):
@@ -38,64 +39,90 @@ def _mask(bits):
     return sum(1 << i for i in bits)
 
 
-def _group(T, topo, core):
-    def here(c):
-        return [d for d in T.cores if topo.host(d) == topo.host(c) and topo.chip(d) == topo.chip(c)]
-
-    pos = here(core).index(core)
-    mate = [d for d in here(core) if d != core][0]
-    rack, cable, diag = {}, {}, {}
-    for d in T.cores:
-        if topo.host(d) == topo.host(core):
-            continue
-        p = here(d).index(d)
-        side = "same" if p == pos else "other"
-        if topo.same_plane(core, d):
-            rack[side] = d
-        elif topo.may_write(core, d):
-            cable[side] = d
-        else:
-            diag[side] = d
-    return mate, rack, cable, diag
+def _place(c, topo):
+    return topo.host(c), topo.chip(c)
 
 
 def rank_program(g, core, T, topo):
-    rank = T.rank_of(core)
-    if rank is None:
+    chips = []
+    for c in T.cores:
+        mine = [r for r in T.cores if _place(r, topo) == _place(c, topo)]
+        if mine not in chips:
+            chips.append(mine)
+    A = [q for q in range(len(chips)) if _place(chips[q][0], topo) == _place(core, topo)]
+    if not A:
+        return
+    A = A[0]
+    R = K = D = None
+    for q in range(len(chips)):
+        if q == A:
+            continue
+        if topo.same_plane(chips[A][0], chips[q][0]):
+            R = q
+        elif topo.may_write(chips[A][0], chips[q][0]):
+            K = q
+        else:
+            D = q
+
+    def helpers(q):
+        r0 = chips[q][0]
+        idle = [c for c in range(WORLD) if _place(c, topo) == _place(r0, topo) and topo.die(c) != topo.die(r0)]
+        return [idle[0], idle[-1]]
+
+    aa, rr, kk = chips[A], chips[R], chips[K]
+    if core not in aa and core not in helpers(A):
         return
     S = T.sem
-    mate, rack, cable, diag = _group(T, topo, core)
 
-    off = _bits(topo.mask(core, rack["same"]) & topo.mask(core, cable["same"]))
-    on = [i for i in _bits(topo.mask(core, mate)) if i not in off]
-    via_switch, via_cable = off[0::2], off[1::2]
-    mate_a, mate_b = on[0::2], on[1::2]
+    off = _bits(topo.mask(core, kk[0]))
+    on = [i for i in _bits(topo.mask(core, [c for c in aa if c != core][0])) if i not in off]
+    off_a, off_b, on_a, on_b = off[0::2], off[1::2], on[0::2], on[1::2]
 
-    own, r, c = rank, T.rank_of(rack["same"]), T.rank_of(cable["same"])
-    ro, co = T.rank_of(rack["other"]), T.rank_of(cable["other"])
-    ds, do, mt = T.rank_of(diag["same"]), T.rank_of(diag["other"]), T.rank_of(mate)
-    codes_due = {mt: len(on), r: len(via_switch), c: len(via_cable), ro: len(on), co: len(on),
-                 ds: len(via_cable), do: len(via_switch)}
-    planes_due = {mt: len(on), r: len(via_switch), c: len(via_cable), ro: len(mate_a), co: len(mate_b),
-                  ds: len(via_cable), do: len(via_switch)}
+    def codes(s, lo=0, hi=C):
+        return T.wq[:, s * C + lo:s * C + hi]
 
-    def codes(e):
-        return T.wq[:, e * C:(e + 1) * C]
-
-    def plane(e):
-        return T.ws[:, e * C:(e + 1) * C]
+    def plane(s):
+        return T.ws[:, s * C:(s + 1) * C]
 
     sent = [0]
 
-    def send(kind, moves):
+    def send(*moves):
         ts = []
-        for e, d, engines in moves:
+        for kind, s, d, engines in moves:
             rid, pid = topo.addr(d, core)
-            ap = codes(e).bitcast(dt.uint8) if kind == "c" else plane(e)
+            if kind == "p":
+                ap, sem = plane(s), "p%d" % s
+            elif kind == "c":
+                ap, sem = codes(s).bitcast(dt.uint8), "c%d" % s
+            elif kind == "lo":
+                ap, sem = codes(s, 0, LO).bitcast(dt.uint8), "h%d" % s
+            else:
+                ap, sem = codes(s, LO, C).bitcast(dt.uint8), "h%d" % s
             ts.append(RemoteDMATransfer(dst_ids=[DstId(rid=rid, pnc=pid)], dma_engine_mask=_mask(engines),
-                                        remote_sem=S["%s%d" % (kind, e)], src=ap, dst=ap))
+                                        remote_sem=S[sem], src=ap, dst=ap))
             sent[0] += len(engines)
         g.remote_dma_fused(ts, local_sem=S.sent)
+
+    if core not in aa:
+        p = helpers(A).index(core)
+        own, r = 2 * A + p, 2 * R + p
+        g.wait_ge(S["p%d" % own], len(on_a))
+        send(("p", own, kk[p], off))
+        g.wait_ge(S["c%d" % r], len(off_a))
+        send(("lo", r, kk[p], off))
+        send(("c", r, aa[0], on_a), ("c", r, aa[1], on_b))
+        g.wait_ge(S["p%d" % r], len(off_a))
+        send(("p", r, kk[p], off))
+        g.wait_ge(S.sent, sent[0])
+        return
+
+    p = aa.index(core)
+    mate = aa[1 - p]
+    own, mt = 2 * A + p, 2 * A + 1 - p
+    r, ro, c, co, d, do = 2 * R + p, 2 * R + 1 - p, 2 * K + p, 2 * K + 1 - p, 2 * D + p, 2 * D + 1 - p
+    codes_due = {mt: ("c", len(on)), r: ("c", len(on_a)), ro: ("c", len(on_a)), c: ("c", len(off_b)), co: ("c", len(on)),
+                 d: ("h", 2 * len(off)), do: ("c", len(off + on))}
+    planes_due = {mt: len(on_b), r: len(off_b), ro: len(on), c: len(off), co: len(on), d: len(off), do: len(off)}
 
     g.sync.dma_start(T.wt[:], T.w[:]).then_inc(S.lw, 16)
     g.sync.dma_start(T.xt[:], T.x[:]).then_inc(S.lx, 16)
@@ -104,37 +131,39 @@ def rank_program(g, core, T, topo):
     g.sync.dma_start(T.y[:], T.yt[:]).then_inc(S.stored, 16)
     g.sync.wait_ge(S.stored, 16)
 
+    h_a, h_r = helpers(A)[p], helpers(R)[p]
     g.wait_ge(S.qw, 1)
-    first = [(own, rack["same"], via_switch), (own, cable["same"], via_cable)]
-    send("c", first)
-    send("p", first)
-    send("c", [(own, mate, on)])
-    send("p", [(own, mate, on)])
-    g.wait_ge(S["c%d" % r], codes_due[r])
-    send("c", [(r, cable["same"], via_cable), (r, mate, on)])
-    g.wait_ge(S["c%d" % c], codes_due[c])
-    send("c", [(c, rack["other"], via_switch), (c, mate, on)])
+    send(("c", own, h_r, off_a), ("c", own, kk[p], off_b))
+    send(("p", own, h_a, on_a), ("p", own, mate, on_b))
+    send(("p", own, h_r, off_a), ("p", own, rr[p], off_b))
+    send(("c", own, mate, on))
+    g.wait_ge(S["c%d" % c], len(off_b))
+    send(("hi", c, rr[p], off))
+    send(("c", c, mate, on))
     g.wait_ge(S["p%d" % r], planes_due[r])
+    send(("p", r, mate, on))
     g.wait_ge(S["p%d" % c], planes_due[c])
-    send("p", [(r, cable["same"], via_cable), (c, rack["other"], via_switch), (r, mate, mate_a), (c, mate, mate_b)])
+    send(("p", c, rr[1 - p], off), ("p", c, mate, on))
+    g.wait_ge(S["h%d" % d], 2 * len(off))
+    send(("c", d, mate, off + on))
     g.wait_ge(S.sent, sent[0])
 
-    order = [own, mt, r, c, ro, co, ds, do]
+    order = [own, mt, c, r, ro, co, d, do]
 
     def bank(k):
         return 512 * ((k + 1) % 8)
 
     g.tensor.wait_ge(S.qx, 2)
     g.tensor.matmul_mx(T.ps[:, 0:C], T.xq[:], T.xs[:], T.rq[:], T.rs[:], True, True).then_inc(S.mr, 1)
-    for k, e in enumerate(order):
-        if e == own:
+    for k, s in enumerate(order):
+        if s == own:
             g.tensor.wait_ge(S.qw, 1)
         else:
-            g.tensor.wait_ge(S["c%d" % e], codes_due[e])
-            g.tensor.wait_ge(S["p%d" % e], planes_due[e])
+            g.tensor.wait_ge(S["%s%d" % (codes_due[s][0], s)], codes_due[s][1])
+            g.tensor.wait_ge(S["p%d" % s], planes_due[s])
         if bank(k) == 0:
             g.tensor.wait_ge(S.lgc, 1)
-        g.tensor.matmul_mx(T.ps[:, bank(k):bank(k) + C], T.xq[:], T.xs[:], codes(e), plane(e), True, True
+        g.tensor.matmul_mx(T.ps[:, bank(k):bank(k) + C], T.xq[:], T.xs[:], codes(s), plane(s), True, True
                            ).then_inc(S["m%d" % k], 1)
 
     V = g.vector
@@ -167,7 +196,8 @@ def rank_program(g, core, T, topo):
         return T.tmp[:, k * C:(k + 1) * C]
 
     g.scalar.wait_ge(S.coef_ok, 1)
-    for k, e in enumerate(order):
+    for k, s in enumerate(order):
+        e = T.rank_of(chips[s // 2][s % 2])
         g.scalar.wait_ge(S["m%d" % k], 1)
         g.scalar.activation(tmp(k), T.ps[:, bank(k):bank(k) + C], ActivationFunctionType.Identity,
                             scale=T.coef[:, e:e + 1]).then_inc(S["a%d" % k], 1)

from concourse.bass import DstId, RemoteDMATransfer
from concourse.mybir import dt, AluOpType, AxisListType, ActivationFunctionType

NE = 8
C = 128
LO = 64
WORLD = 512
SCRATCH = {
    "wt": ("sbuf", [128, 512], "bfloat16"),
    "xt": ("sbuf", [128, 512], "bfloat16"),
    "rtt": ("sbuf", [128, 512], "bfloat16"),
    "wq": ("sbuf", [128, NE * C], "float8_e4m3fn_x4"),
    "ws": ("sbuf", [128, NE * C], "uint8"),
    "xq": ("sbuf", [128, C], "float8_e4m3fn_x4"),
    "xs": ("sbuf", [128, C], "uint8"),
    "rq": ("sbuf", [128, C], "float8_e4m3fn_x4"),
    "rs": ("sbuf", [128, C], "uint8"),
    "ps": ("psum", [128, 512 * 8], "float32"),
    "lg": ("sbuf", [128, NE], "float32"),
    "pen": ("sbuf", [128, NE], "float32"),
    "low": ("sbuf", [128, NE], "float32"),
    "sel": ("sbuf", [128, NE], "float32"),
    "coef": ("sbuf", [128, NE], "float32"),
    "m1": ("sbuf", [128, 1], "float32"),
    "m2": ("sbuf", [128, 1], "float32"),
    "tmp": ("sbuf", [128, NE * C], "float32"),
    "acc": ("sbuf", [128, C], "float32"),
    "yt": ("sbuf", [128, C], "float32"),
}
SEMAPHORES = (["lw", "lx", "lr", "qw", "qx", "mr", "lgc", "v", "coef_ok", "yv", "stored", "sent"]
              + ["%s%d" % (k, e) for k in "chpma" for e in range(NE)])


def _bits(m):
    return [i for i in range(m.bit_length()) if (m >> i) & 1]


def _mask(bits):
    return sum(1 << i for i in bits)


def _place(c, topo):
    return topo.host(c), topo.chip(c)


def rank_program(g, core, T, topo):
    chips = []
    for c in T.cores:
        mine = [r for r in T.cores if _place(r, topo) == _place(c, topo)]
        if mine not in chips:
            chips.append(mine)
    A = [q for q in range(len(chips)) if _place(chips[q][0], topo) == _place(core, topo)]
    if not A:
        return
    A = A[0]
    R = K = D = None
    for q in range(len(chips)):
        if q == A:
            continue
        if topo.same_plane(chips[A][0], chips[q][0]):
            R = q
        elif topo.may_write(chips[A][0], chips[q][0]):
            K = q
        else:
            D = q

    def helpers(q):
        r0 = chips[q][0]
        idle = [c for c in range(WORLD) if _place(c, topo) == _place(r0, topo) and topo.die(c) != topo.die(r0)]
        return [idle[0], idle[-1]]

    aa, rr, kk = chips[A], chips[R], chips[K]
    if core not in aa and core not in helpers(A):
        return
    S = T.sem

    off = _bits(topo.mask(core, kk[0]))
    on = [i for i in _bits(topo.mask(core, [c for c in aa if c != core][0])) if i not in off]
    off_a, off_b, on_a, on_b = off[0::2], off[1::2], on[0::2], on[1::2]

    def codes(s, lo=0, hi=C):
        return T.wq[:, s * C + lo:s * C + hi]

    def plane(s):
        return T.ws[:, s * C:(s + 1) * C]

    sent = [0]

    def send(*moves):
        ts = []
        for kind, s, d, engines in moves:
            rid, pid = topo.addr(d, core)
            if kind == "p":
                ap, sem = plane(s), "p%d" % s
            elif kind == "c":
                ap, sem = codes(s).bitcast(dt.uint8), "c%d" % s
            elif kind == "lo":
                ap, sem = codes(s, 0, LO).bitcast(dt.uint8), "h%d" % s
            else:
                ap, sem = codes(s, LO, C).bitcast(dt.uint8), "h%d" % s
            ts.append(RemoteDMATransfer(dst_ids=[DstId(rid=rid, pnc=pid)], dma_engine_mask=_mask(engines),
                                        remote_sem=S[sem], src=ap, dst=ap))
            sent[0] += len(engines)
        g.remote_dma_fused(ts, local_sem=S.sent)

    if core not in aa:
        p = helpers(A).index(core)
        own, r = 2 * A + p, 2 * R + p
        g.wait_ge(S["p%d" % own], len(on_a))
        send(("p", own, kk[p], off))
        g.wait_ge(S["c%d" % r], len(off_a))
        send(("lo", r, kk[p], off))
        send(("c", r, aa[0], on_a), ("c", r, aa[1], on_b))
        g.wait_ge(S["p%d" % r], len(off_a))
        send(("p", r, kk[p], off))
        g.wait_ge(S.sent, sent[0])
        return

    p = aa.index(core)
    mate = aa[1 - p]
    own, mt = 2 * A + p, 2 * A + 1 - p
    r, ro, c, co, d, do = 2 * R + p, 2 * R + 1 - p, 2 * K + p, 2 * K + 1 - p, 2 * D + p, 2 * D + 1 - p
    codes_due = {mt: ("c", len(on)), r: ("c", len(on_a)), ro: ("c", len(on_a)), c: ("c", len(off_b)), co: ("c", len(on)),
                 d: ("h", 2 * len(off)), do: ("c", len(off + on))}
    planes_due = {mt: len(on_b), r: len(off_b), ro: len(on), c: len(off), co: len(on), d: len(off), do: len(off)}

    g.sync.dma_start(T.wt[:], T.w[:]).then_inc(S.lw, 16)
    g.sync.dma_start(T.xt[:], T.x[:]).then_inc(S.lx, 16)
    g.sync.dma_start(T.rtt[:], T.rt[:]).then_inc(S.lr, 16)
    g.sync.wait_ge(S.yv, 1)
    g.sync.dma_start(T.y[:], T.yt[:]).then_inc(S.stored, 16)
    g.sync.wait_ge(S.stored, 16)

    h_a, h_r = helpers(A)[p], helpers(R)[p]
    g.wait_ge(S.qw, 1)
    send(("c", own, h_r, off_a), ("c", own, kk[p], off_b))
    send(("p", own, h_a, on_a), ("p", own, mate, on_b))
    send(("p", own, h_r, off_a), ("p", own, rr[p], off_b))
    send(("c", own, mate, on))
    g.wait_ge(S["c%d" % c], len(off_b))
    send(("hi", c, rr[p], off))
    send(("c", c, mate, on))
    g.wait_ge(S["p%d" % r], planes_due[r])
    send(("p", r, mate, on))
    g.wait_ge(S["p%d" % c], planes_due[c])
    send(("p", c, rr[1 - p], off), ("p", c, mate, on))
    g.wait_ge(S["h%d" % d], 2 * len(off))
    send(("c", d, mate, off + on))
    g.wait_ge(S.sent, sent[0])

    order = [own, mt, c, r, ro, co, d, do]

    def bank(k):
        return 512 * ((k + 1) % 8)

    g.tensor.wait_ge(S.qx, 2)
    g.tensor.matmul_mx(T.ps[:, 0:C], T.xq[:], T.xs[:], T.rq[:], T.rs[:], True, True).then_inc(S.mr, 1)
    for k, s in enumerate(order):
        if s == own:
            g.tensor.wait_ge(S.qw, 1)
        else:
            g.tensor.wait_ge(S["%s%d" % (codes_due[s][0], s)], codes_due[s][1])
            g.tensor.wait_ge(S["p%d" % s], planes_due[s])
        if bank(k) == 0:
            g.tensor.wait_ge(S.lgc, 1)
        g.tensor.matmul_mx(T.ps[:, bank(k):bank(k) + C], T.xq[:], T.xs[:], codes(s), plane(s), True, True
                           ).then_inc(S["m%d" % k], 1)

    V = g.vector
    V.wait_ge(S.lw, 16)
    V.quantize_mx(codes(own), plane(own), T.wt[:]).then_inc(S.qw, 1)
    V.wait_ge(S.lx, 16)
    V.quantize_mx(T.xq[:], T.xs[:], T.xt[:]).then_inc(S.qx, 1)
    V.wait_ge(S.lr, 16)
    V.quantize_mx(T.rq[:], T.rs[:], T.rtt[:]).then_inc(S.qx, 1)

    nv = [0]

    def step(ins):
        nv[0] += 1
        ins.then_inc(S.v, 1)
        V.wait_ge(S.v, nv[0])

    X = AxisListType.X
    V.wait_ge(S.mr, 1)
    V.tensor_copy(T.lg[:], T.ps[:, 0:NE]).then_inc(S.lgc, 1)
    V.wait_ge(S.lgc, 1)
    step(V.tensor_reduce(T.m1[:], T.lg[:], X, AluOpType.max))
    step(V.tensor_scalar(T.pen[:], T.lg[:], T.m1[:], -1e29, AluOpType.is_ge, AluOpType.mult))
    step(V.tensor_tensor(T.low[:], T.lg[:], T.pen[:], AluOpType.add))
    step(V.tensor_reduce(T.m2[:], T.low[:], X, AluOpType.max))
    step(V.tensor_scalar(T.sel[:], T.lg[:], T.m2[:], None, AluOpType.is_ge))
    V.tensor_tensor(T.coef[:], T.sel[:], T.lg[:], AluOpType.mult).then_inc(S.coef_ok, 1)

    def tmp(k):
        return T.tmp[:, k * C:(k + 1) * C]

    g.scalar.wait_ge(S.coef_ok, 1)
    for k, s in enumerate(order):
        e = T.rank_of(chips[s // 2][s % 2])
        g.scalar.wait_ge(S["m%d" % k], 1)
        g.scalar.activation(tmp(k), T.ps[:, bank(k):bank(k) + C], ActivationFunctionType.Identity,
                            scale=T.coef[:, e:e + 1]).then_inc(S["a%d" % k], 1)
    V.wait_ge(S.a0, 1)
    for k in range(1, NE):
        V.wait_ge(S["a%d" % k], 1)
        a = tmp(0) if k == 1 else T.acc[:]
        if k < NE - 1:
            step(V.tensor_tensor(T.acc[:], a, tmp(k), AluOpType.add))
        else:
            V.tensor_tensor(T.yt[:], a, tmp(k), AluOpType.add).then_inc(S.yv, 1)
